import numpy as np
import ml_dtypes


def mxq(x, axis, fmt="e4m3"):
    dtype, down = {"e4m3": (ml_dtypes.float8_e4m3fn, 7), "e5m2": (ml_dtypes.float8_e5m2, 14)}[fmt]
    v = np.moveaxis(np.asarray(x, np.float32).astype(ml_dtypes.bfloat16).astype(np.float64), axis, -1)
    blocks = v.reshape(v.shape[:-1] + (-1, 32))
    amax = np.abs(blocks).max(-1, keepdims=True)
    byte = np.maximum(np.where(amax > 0, np.frexp(amax)[1] - 1 + 127, 0) - down, 1)
    scale = np.exp2(byte - 127.0)
    codes = (blocks / scale).astype(np.float32).astype(dtype).astype(np.float64)
    return np.moveaxis((codes * scale).reshape(v.shape), -1, axis)


WIDE = False


def mx_kscale(k):
    if not WIDE:
        return np.ones(k)
    levels = np.array([10, -10, 5, -5, 0])
    if k % 512:
        return np.exp2(np.random.permutation(np.resize(levels, k // 32))).repeat(32)
    a = np.empty((k // 512, 16))
    for p in range(k // 512):
        a[p, :8] = np.random.permutation(np.resize(levels, 8))
        for g in range(8):
            far = levels[np.abs(levels - a[p, g]) >= 10]
            a[p, g + 8] = far[np.random.randint(len(far))]
    return np.exp2(a.ravel()).repeat(32)


def f64(x):
    return np.asarray(x).astype(np.float64)


def striped(idx):
    return np.tile(idx.reshape(-1, 16).T, (8, 1)).astype(np.uint16)


def unstriped(offs):
    return offs[:16].T.reshape(-1).astype(np.int64)


def striped8(idx):
    return np.concatenate([x.reshape(-1, 16).T for x in idx]).astype(np.uint16)


def runs(offs, k):
    lists = np.stack([offs[16 * r : 16 * r + 16].T.reshape(-1) for r in range(8)]).astype(np.int64)
    return lists[np.arange(k) % 512 // 64]


def pack_weight(w):
    k, n = w.shape
    w = f64(np.asarray(w, np.float32).astype(ml_dtypes.bfloat16)).reshape(k // 32, 32, n)
    amax = np.abs(w).max(1)
    byte = np.clip(np.where(amax > 0, np.frexp(amax)[1] - 1 + 127 - 7, 1), 1, 254)
    scaled = (w * np.exp2(127.0 - byte)[:, None, :]).reshape(k, n).astype(np.float32)
    words = np.ascontiguousarray(scaled.reshape(k // 512, 128, 4, n).transpose(0, 1, 3, 2)).astype(ml_dtypes.float8_e4m3fn).view(np.uint8)
    return words, np.ascontiguousarray(byte.astype(np.uint8).reshape(k // 512, 16, n))


def unpack_weight(words, scales):
    g, p, n, _ = words.shape
    vals = np.ascontiguousarray(words).view(ml_dtypes.float8_e4m3fn).astype(np.float64) * np.repeat(np.exp2(scales.astype(np.float64) - 127.0), 8, axis=1)[..., None]
    return vals.transpose(0, 1, 3, 2).reshape(g * 512, n)


def sigmoid(v):
    return 1.0 / (1.0 + np.exp(-np.maximum(v, -700.0)))

def planes(y):
    n, m = y.shape
    v = y.astype(np.float32).astype(ml_dtypes.bfloat16).astype(np.float64).reshape(n // 32, 32, m)
    top = np.abs(v).max(1)
    byte = np.clip(np.where(top > 0, np.frexp(top)[1] - 1 + 127 - 7, 1), 1, 254)
    codes = (v * np.exp2(127.0 - byte)[:, None, :]).reshape(n, m).astype(np.float32).astype(ml_dtypes.float8_e4m3fn).view(np.uint8)
    words = codes.reshape(n // 512, 128, 4, m).transpose(0, 1, 3, 2)
    return np.ascontiguousarray(words), np.ascontiguousarray(byte.astype(np.uint8).reshape(n // 512, 16, m))


K, T, S, G, H, J = 512, 2048, 512, 2048, 512, 512


def setup_inputs():
    n = np.random.standard_normal
    s = mx_kscale(K)[:, None]
    packed_xT = pack_weight(n((K, T)) * s)
    packed_dT = pack_weight(n((K, G)) / s)
    return {
        "x_words": packed_xT[0],
        "x_scales": packed_xT[1],
        "d_words": packed_dT[0],
        "d_scales": packed_dT[1],
        "tab": n((H, J)).astype(np.float32),
        "sl": np.random.uniform(1.0, 2.0, (H, 1)).astype(np.float32),
        "th": (0.5 * n((H, 1))).astype(np.float32),
        "gs": (np.random.uniform(0.5, 1.5, (K, 1)) * s).astype(np.float32),
        "tau": np.random.uniform(0.3, 0.9, (H, 1)).astype(np.float32),
        "offs": striped(np.random.permutation(T)[:S]),
        "k1": striped8(np.random.randint(0, G, (8, H))),
        "n1": striped(np.random.randint(0, J, S)),
        "n2": striped(np.random.permutation(S)),
        "n3": striped8(np.stack([np.random.permutation(S) for _ in range(8)])),
    }


def reference(x_words, x_scales, d_words, d_scales, tab, sl, th, gs, tau, offs, k1, n1, n2, n3):
    d_k1 = unpack_weight(d_words, d_scales)[np.arange(K)[:, None], runs(k1, K)]
    xq = unpack_weight(x_words, x_scales)[:, unstriped(offs)]
    h = 0.0625 * (d_k1.T @ xq)
    sg = sigmoid(f64(sl) * (f64(tab)[:, unstriped(n1)] - f64(th)))
    z = f64(gs) * (h * sg - (0.5 * h[:, unstriped(n2)]))
    h2 = 0.0625 * ((d_k1.T @ mxq(z, 0, "e4m3")))
    top = h2.max(axis=1, keepdims=True)
    ea = np.exp(f64(tau) * (h2[np.arange(H)[:, None], runs(n3, H)] - top))
    out_0 = 2.0 * (h2 * ea)
    return (out_0,) + planes(out_0)

@@ -1,0 +1,245 @@
+from contextlib import ExitStack
+
+import concourse.mybir as mybir
+
+F32 = mybir.dt.float32
+BF16 = mybir.dt.bfloat16
+I32 = mybir.dt.int32
+U32 = mybir.dt.uint32
+U16 = mybir.dt.uint16
+U8 = mybir.dt.uint8
+FP8X4 = mybir.dt.float8_e4m3fn_x4
+ALU = mybir.AluOpType
+ACT = mybir.ActivationFunctionType
+
+P = 128
+PACK = 4
+TABLE = 2048
+S = 512
+HALF = S // 2
+FLOPS = 2 * 2 * 512 * 512 * 512
+
+HALVES = ((0, HALF), (HALF, S))
+OUT_CHUNKS = ((0, 256), (256, 384), (384, 512))
+
+
+def entries(lst, lo, hi):
+    return lst[:, lo // 16 : hi // 16]
+
+
+def tile_picked_ringekdepk_none_po_kernel(
+    tc, x_words, x_scales, d_words, d_scales, tab, sl, th, gs, tau, offs, k1, n1, n2, n3, out_0, out_1, out_2
+):
+    nc = tc.nc
+    with ExitStack() as ctx:
+        sb = ctx.enter_context(tc.tile_pool(name="sb", bufs=1))
+        ps = ctx.enter_context(tc.psum_pool(name="ps", bufs=1))
+
+        def load_list(src, name):
+            lst = sb.tile([P, S // 16], U16, name=name)
+            nc.sync.dma_start(lst[:], src)
+            return lst
+
+        def load_words(src, name):
+            words = sb.tile([P, TABLE], I32, name=name, align_bytes=64)
+            nc.sync.dma_start(words[:], src[0].rearrange("p c r -> p (c r)").bitcast(I32))
+            return words
+
+        tab_rows = tab.rearrange("(p t) j -> p t j", t=PACK)
+
+        def load_tab(t):
+            rows = sb.tile([P, S], F32, name=f"tab{t}", align_bytes=64)
+            nc.sync.dma_start(rows[:], tab_rows[:, t, :])
+            return rows
+
+        def load_column(src, name, queue):
+            col = sb.tile([P, PACK], F32, name=name, tag=name, align_bytes=64)
+            queue.dma_start(col[:], src.rearrange("(p t) o -> p (t o)", t=PACK))
+            return col
+
+        def load_scales(src, name):
+            table = sb.tile([P, TABLE], U8, name=name, align_bytes=64)
+            rows = src[0].bitcast(I32)
+            nc.sync.dma_start(table[:].bitcast(I32), rows.unsqueeze(1).to_broadcast([16, 8, TABLE // 4]))
+            return table
+
+        k1_t = load_list(k1, "k1_t")
+        d_sc_table = load_scales(d_scales, "d_sc_table")
+        offs_t = load_list(offs, "offs_t")
+        x_sc_table = load_scales(x_scales, "x_sc_table")
+        n1_t = load_list(n1, "n1_t")
+        sl_t = load_column(sl, "sl_t", nc.sync)
+        th_t = load_column(th, "th_t", nc.sync)
+        d_table = load_words(d_words, "d_table")
+        tabs = [load_tab(0)]
+        n2_t = load_list(n2, "n2_t")
+        x_table = load_words(x_words, "x_table")
+        tabs.extend(load_tab(t) for t in range(1, PACK))
+        n3_t = load_list(n3, "n3_t")
+        gs_t = load_column(gs, "gs_t", nc.gpsimd)
+        tau_t = load_column(tau, "tau_t", nc.gpsimd)
+
+        d_sc_picked = sb.tile([P, S], U8, align_bytes=64)
+        nc.vector.tensor_copy(d_sc_picked[:], d_sc_table[:].indirect(k1_t[:]))
+        spread_sc = sb.tile([P, 2 * S], U8, align_bytes=64)
+        nc.vector.tensor_copy(
+            spread_sc[:, :S].rearrange("p (t m) -> p t m", t=PACK), d_sc_picked[:].rearrange("p (m t) -> p t m", t=PACK)
+        )
+        x_sc_picked = sb.tile([P, S], U8, align_bytes=64)
+        nc.vector.tensor_copy(x_sc_picked[:], x_sc_table[:].indirect(offs_t[:]))
+        nc.vector.tensor_copy(spread_sc[:, S:].bitcast(I32), x_sc_picked[:].bitcast(I32))
+        packed_sc = sb.tile([P, 2 * S], U8, align_bytes=64)
+        nc.vector.tensor_copy(packed_sc[:].bitcast(I32), spread_sc[:].bitcast(I32))
+        for r in range(1, 4):
+            nc.scalar.dma_start(packed_sc[:].bitcast(I32)[r:P:32, :], spread_sc[:].bitcast(I32)[8 * r : P : 32, :])
+        d_sc = packed_sc[:, :S]
+        x_sc = packed_sc[:, S:]
+
+        d_picked = sb.tile([P, S], U32, align_bytes=64)
+        nc.vector.tensor_copy(d_picked[:], d_table[:].bitcast(U32).indirect(k1_t[:]))
+        d_codes = sb.tile([P, S], U32, align_bytes=64)
+        nc.vector.tensor_copy(
+            d_codes[:].rearrange("p (t m) -> p t m", t=PACK), d_picked[:].rearrange("p (m t) -> p t m", t=PACK)
+        )
+
+        sig_bias = sb.tile([P, PACK], F32)
+        minus_th = sb.tile([P, PACK], F32)
+        nc.scalar.activation(minus_th[:], th_t[:], ACT.Copy, scale=-1.0)
+        nc.gpsimd.tensor_tensor(sig_bias[:], sl_t[:], minus_th[:], ALU.mult)
+        gs16 = sb.tile([P, PACK], F32)
+        nc.gpsimd.tensor_scalar(gs16[:], gs_t[:], 0.0625, 0.0, ALU.mult, ALU.add)
+
+        x_codes = sb.tile([P, S], U32, align_bytes=64)
+        nc.vector.tensor_copy(x_codes[:], x_table[:].bitcast(U32).indirect(offs_t[:]))
+
+        def product(bank, t, codes, scales):
+            cols = slice(t * P, (t + 1) * P)
+            nc.tensor.matmul_mx(
+                out=bank,
+                lhsT=d_codes[:, cols].bitcast(FP8X4),
+                lhsT_scale=d_sc[:, cols],
+                rhs=codes.bitcast(FP8X4),
+                rhs_scale=scales,
+                start=True,
+                stop=True,
+            )
+
+        sg = [sb.tile([P, PACK, HALF], F32, name=f"sg{c}", align_bytes=64) for c in range(2)]
+
+        def sigmoid(c, t):
+            lo, hi = HALVES[c]
+            nc.scalar.activation(
+                sg[c][:, t, :],
+                tabs[t][:].indirect(entries(n1_t, lo, hi)),
+                ACT.Sigmoid,
+                bias=sig_bias[:, t : t + 1],
+                scale=sl_t[:, t : t + 1],
+            )
+
+        sigmoid(0, 0)
+        sigmoid(1, 0)
+        for t in range(1, PACK):
+            sigmoid(0, t)
+
+        h_banks = []
+        half_h = []
+        for t in range(PACK):
+            bank = ps.tile([P, S], F32, name=f"h{t}", tag=f"bank{t}")
+            product(bank[:], t, x_codes[:], x_sc)
+            h_banks.append(bank)
+        for t in range(PACK):
+            window = sb.tile([P, S], F32, name=f"half_h{t}", align_bytes=64)
+            nc.vector.tensor_scalar(window[:], h_banks[t][:], gs_t[:, t : t + 1], 0.03125, ALU.mult, ALU.mult)
+            half_h.append(window)
+
+        z_codes = sb.tile([P, S], U32, align_bytes=64)
+        z_sc = sb.tile([P, S], U8, align_bytes=64)
+        h2_banks = []
+        for c, (lo, hi) in enumerate(HALVES):
+            fetched = sb.tile([P, PACK, HALF], F32, name=f"fetched{c}", tag=("fetched0", "gs_t")[c], align_bytes=64)
+            gated = sb.tile([P, PACK, HALF], F32, name=f"gated{c}", align_bytes=64)
+            for t in range(PACK):
+                if c == 1 and t > 0:
+                    sigmoid(c, t)
+                nc.scalar.activation(fetched[:, t, :], half_h[t][:].indirect(entries(n2_t, lo, hi)), ACT.Copy)
+                nc.vector.scalar_tensor_tensor(
+                    gated[:, t, :], h_banks[t][:, lo:hi], gs16[:, t : t + 1], sg[c][:, t, :], ALU.mult, ALU.mult
+                )
+            z = sb.tile([P, HALF, PACK], BF16, name=f"z{c}", align_bytes=64)
+            nc.vector.tensor_tensor(
+                z[:].rearrange("p (c i) t -> p c t i", i=4),
+                gated[:].rearrange("p t (c i) -> p c t i", i=4),
+                fetched[:].rearrange("p t (c i) -> p c t i", i=4),
+                ALU.subtract,
+            )
+            nc.vector.quantize_mx(
+                out=z_codes[:, lo:hi].bitcast(FP8X4), scales=z_sc[:, lo:hi], in_=z[:].rearrange("p j t -> p (j t)")
+            )
+            banks = []
+            for t in range(PACK):
+                bank = ps.tile([P, HALF], F32, name=f"h2_{c}_{t}", tag=f"bank{(1 - c) * PACK + t}")
+                product(bank[:], t, z_codes[:, lo:hi], z_sc[:, lo:hi])
+                banks.append(bank)
+            h2_banks.append(banks)
+
+        top_first = sb.tile([P, PACK], F32)
+        top = sb.tile([P, PACK], F32, tag="top", align_bytes=64)
+        exp_bias = sb.tile([P, PACK], F32)
+        ea = [sb.tile([P, PACK, hi - lo], F32, name=f"ea{c}", align_bytes=64) for c, (lo, hi) in enumerate(OUT_CHUNKS[:2])]
+        y = [sb.tile([P, PACK, hi - lo], F32, name=f"y{c}", align_bytes=64) for c, (lo, hi) in enumerate(OUT_CHUNKS)]
+        h2 = [sb.tile([P, S], F32, name=f"h2_{t}", align_bytes=64) for t in range(PACK)]
+
+        def exp_and_multiply(c, t):
+            lo, hi = OUT_CHUNKS[c]
+            nc.scalar.activation(
+                ea[c][:, t, :],
+                h2[t][:].indirect(entries(n3_t, lo, hi)),
+                ACT.Exp,
+                bias=exp_bias[:, t : t + 1],
+                scale=tau_t[:, t : t + 1],
+            )
+            bank = h2_banks[lo // HALF][t]
+            nc.vector.scalar_tensor_tensor(
+                y[c][:, t, :], bank[:, lo % HALF : lo % HALF + hi - lo], 0.125, ea[c][:, t, :], ALU.mult, ALU.mult
+            )
+
+        for t in range(PACK):
+            col = slice(t, t + 1)
+            nc.vector.tensor_scalar(
+                h2[t][:, :HALF], h2_banks[0][t][:], 0.0625, None, ALU.mult, ALU.max, accum_out=top_first[:, col]
+            )
+            nc.vector.tensor_scalar(
+                h2[t][:, HALF:], h2_banks[1][t][:], 0.0625, top_first[:, col], ALU.mult, ALU.max, accum_out=top[:, col]
+            )
+            nc.vector.tensor_scalar(exp_bias[:, col], top[:, col], tau_t[:, col], -1.0, ALU.mult, ALU.mult)
+        for t in range(PACK):
+            exp_and_multiply(0, t)
+            exp_and_multiply(1, t)
+
+        y_codes = sb.tile([P, S], U32, align_bytes=64)
+        y_sc = sb.tile([P, S], U8, align_bytes=64)
+        out_rows = out_0.rearrange("(p t) j -> p t j", t=PACK)
+        out_words = out_1[0].rearrange("p c r -> p (c r)").bitcast(I32)
+
+        def hand_out(c):
+            lo, hi = OUT_CHUNKS[c]
+            nc.sync.dma_start(out_rows[:, :, lo:hi], y[c][:])
+            rounded = sb.tile([P, hi - lo, PACK], BF16, name=f"rounded{c}", align_bytes=64)
+            nc.vector.tensor_copy(
+                rounded[:].rearrange("p (c i) t -> p c t i", i=4), y[c][:].rearrange("p t (c i) -> p c t i", i=4)
+            )
+            nc.vector.quantize_mx(
+                out=y_codes[:, lo:hi].bitcast(FP8X4), scales=y_sc[:, lo:hi], in_=rounded[:].rearrange("p j t -> p (j t)")
+            )
+            nc.sync.dma_start(out_words[:, lo:hi], y_codes[:, lo:hi].bitcast(I32))
+
+        hand_out(0)
+        ea.append(sb.tile([P, PACK, 128], F32, name="ea2", tag="top", align_bytes=64))
+        for t in range(PACK):
+            exp_and_multiply(2, t)
+        hand_out(1)
+        hand_out(2)
+        out_sc_rows = out_2[0].bitcast(I32)
+        for q in range(4):
+            queue = nc.scalar if q % 2 == 0 else nc.sync
+            queue.dma_start(out_sc_rows[4 * q : 4 * q + 4, :], y_sc[:].bitcast(I32)[32 * q : 32 * q + 4, :])

@@ -33,6 +33,7 @@ def tile_picked_ringekdepk_none_po_kernel(
     nc = tc.nc
     with ExitStack() as ctx:
         sb = ctx.enter_context(tc.tile_pool(name="sb", bufs=1))
+        reuse = ctx.enter_context(tc.tile_pool(name="reuse", bufs=1))
         ps = ctx.enter_context(tc.psum_pool(name="ps", bufs=1))
 
         def load_list(src, name):
@@ -40,15 +41,15 @@ def tile_picked_ringekdepk_none_po_kernel(
             nc.sync.dma_start(lst[:], src)
             return lst
 
-        def load_words(src, name):
-            words = sb.tile([P, TABLE], I32, name=name, align_bytes=64)
+        def load_words(src, name, offset):
+            words = reuse.tile([P, TABLE], I32, name=name, align_bytes=64, offset=offset)
             nc.sync.dma_start(words[:], src[0].rearrange("p c r -> p (c r)").bitcast(I32))
             return words
 
         tab_rows = tab.rearrange("(p t) j -> p t j", t=PACK)
 
-        def load_tab(t):
-            rows = sb.tile([P, S], F32, name=f"tab{t}", align_bytes=64)
+        def load_tab(t, offset):
+            rows = reuse.tile([P, S], F32, name=f"tab{t}", align_bytes=64, offset=offset)
             nc.sync.dma_start(rows[:], tab_rows[:, t, :])
             return rows
 
@@ -70,45 +71,49 @@ def tile_picked_ringekdepk_none_po_kernel(
         n1_t = load_list(n1, "n1_t")
         sl_t = load_column(sl, "sl_t", nc.sync)
         th_t = load_column(th, "th_t", nc.sync)
-        d_table = load_words(d_words, "d_table")
-        tabs = [load_tab(0)]
+        d_table = load_words(d_words, "d_table", 0)
+        tabs = [load_tab(0, 8 * TABLE)]
         n2_t = load_list(n2, "n2_t")
-        x_table = load_words(x_words, "x_table")
-        tabs.extend(load_tab(t) for t in range(1, PACK))
         n3_t = load_list(n3, "n3_t")
+        x_table = load_words(x_words, "x_table", 4 * TABLE)
         gs_t = load_column(gs, "gs_t", nc.gpsimd)
         tau_t = load_column(tau, "tau_t", nc.gpsimd)
 
         d_sc_picked = sb.tile([P, S], U8, align_bytes=64)
         nc.vector.tensor_copy(d_sc_picked[:], d_sc_table[:].indirect(k1_t[:]))
-        spread_sc = sb.tile([P, 2 * S], U8, align_bytes=64)
-        nc.vector.tensor_copy(
-            spread_sc[:, :S].rearrange("p (t m) -> p t m", t=PACK), d_sc_picked[:].rearrange("p (m t) -> p t m", t=PACK)
-        )
         x_sc_picked = sb.tile([P, S], U8, align_bytes=64)
         nc.vector.tensor_copy(x_sc_picked[:], x_sc_table[:].indirect(offs_t[:]))
+        spread_sc = sb.tile([P, 2 * S], U8, align_bytes=64)
+        nc.vector.tensor_copy(
+            spread_sc[:, :S].rearrange("p (t c i) -> p c t i", t=PACK, i=16),
+            d_sc_picked[:].rearrange("p (c i t) -> p c t i", t=PACK, i=16),
+        )
         nc.vector.tensor_copy(spread_sc[:, S:].bitcast(I32), x_sc_picked[:].bitcast(I32))
-        packed_sc = sb.tile([P, 2 * S], U8, align_bytes=64)
-        nc.vector.tensor_copy(packed_sc[:].bitcast(I32), spread_sc[:].bitcast(I32))
-        for r in range(1, 4):
-            nc.scalar.dma_start(packed_sc[:].bitcast(I32)[r:P:32, :], spread_sc[:].bitcast(I32)[8 * r : P : 32, :])
-        d_sc = packed_sc[:, :S]
-        x_sc = packed_sc[:, S:]
+        packed_sc = sb.tile([P, 2 * S // 4], I32, align_bytes=64)
+        nc.gpsimd.memset(packed_sc[:], 0)
+        for q in range(4):
+            nc.sync.dma_start(packed_sc[32 * q : 32 * q + 4, :], spread_sc[32 * q : 32 * q + 32 : 8, :].bitcast(I32))
+        d_sc = packed_sc[:].bitcast(U8)[:, :S]
+        x_sc = packed_sc[:].bitcast(U8)[:, S:]
 
         d_picked = sb.tile([P, S], U32, align_bytes=64)
         nc.vector.tensor_copy(d_picked[:], d_table[:].bitcast(U32).indirect(k1_t[:]))
+        tabs.extend(load_tab(t, 4 * S * (t - 1)) for t in range(1, PACK))
         d_codes = sb.tile([P, S], U32, align_bytes=64)
         nc.vector.tensor_copy(
-            d_codes[:].rearrange("p (t m) -> p t m", t=PACK), d_picked[:].rearrange("p (m t) -> p t m", t=PACK)
+            d_codes[:].rearrange("p (t c i) -> p c t i", t=PACK, i=4),
+            d_picked[:].rearrange("p (c i t) -> p c t i", t=PACK, i=4),
         )
 
         sig_bias = sb.tile([P, PACK], F32)
         minus_th = sb.tile([P, PACK], F32)
-        nc.scalar.activation(minus_th[:], th_t[:], ACT.Copy, scale=-1.0)
+        nc.gpsimd.tensor_scalar(minus_th[:], th_t[:], -1.0, 0.0, ALU.mult, ALU.add)
         nc.gpsimd.tensor_tensor(sig_bias[:], sl_t[:], minus_th[:], ALU.mult)
         gs16 = sb.tile([P, PACK], F32)
         nc.gpsimd.tensor_scalar(gs16[:], gs_t[:], 0.0625, 0.0, ALU.mult, ALU.add)
 
+        minus_tau = sb.tile([P, PACK], F32)
+        nc.scalar.activation(minus_tau[:], tau_t[:], ACT.Copy, scale=-1.0)
         x_codes = sb.tile([P, S], U32, align_bytes=64)
         nc.vector.tensor_copy(x_codes[:], x_table[:].bitcast(U32).indirect(offs_t[:]))
 
@@ -124,22 +129,16 @@ def tile_picked_ringekdepk_none_po_kernel(
                 stop=True,
             )
 
-        sg = [sb.tile([P, PACK, HALF], F32, name=f"sg{c}", align_bytes=64) for c in range(2)]
-
-        def sigmoid(c, t):
-            lo, hi = HALVES[c]
-            nc.scalar.activation(
-                sg[c][:, t, :],
-                tabs[t][:].indirect(entries(n1_t, lo, hi)),
-                ACT.Sigmoid,
-                bias=sig_bias[:, t : t + 1],
-                scale=sl_t[:, t : t + 1],
-            )
-
-        sigmoid(0, 0)
-        sigmoid(1, 0)
-        for t in range(1, PACK):
-            sigmoid(0, t)
+        sg = sb.tile([P, PACK, S], F32, align_bytes=64)
+        for t in range(PACK):
+            for lo, hi in HALVES:
+                nc.scalar.activation(
+                    sg[:, t, lo:hi],
+                    tabs[t][:].indirect(entries(n1_t, lo, hi)),
+                    ACT.Sigmoid,
+                    bias=sig_bias[:, t : t + 1],
+                    scale=sl_t[:, t : t + 1],
+                )
 
         h_banks = []
         half_h = []
@@ -151,24 +150,23 @@ def tile_picked_ringekdepk_none_po_kernel(
             window = sb.tile([P, S], F32, name=f"half_h{t}", align_bytes=64)
             nc.vector.tensor_scalar(window[:], h_banks[t][:], gs_t[:, t : t + 1], 0.03125, ALU.mult, ALU.mult)
             half_h.append(window)
+        gated = sb.tile([P, PACK, S], F32, align_bytes=64)
+        for t in range(PACK):
+            nc.vector.scalar_tensor_tensor(
+                gated[:, t, :], h_banks[t][:], gs16[:, t : t + 1], sg[:, t, :], ALU.mult, ALU.mult
+            )
 
         z_codes = sb.tile([P, S], U32, align_bytes=64)
         z_sc = sb.tile([P, S], U8, align_bytes=64)
         h2_banks = []
         for c, (lo, hi) in enumerate(HALVES):
             fetched = sb.tile([P, PACK, HALF], F32, name=f"fetched{c}", tag=("fetched0", "gs_t")[c], align_bytes=64)
-            gated = sb.tile([P, PACK, HALF], F32, name=f"gated{c}", align_bytes=64)
             for t in range(PACK):
-                if c == 1 and t > 0:
-                    sigmoid(c, t)
                 nc.scalar.activation(fetched[:, t, :], half_h[t][:].indirect(entries(n2_t, lo, hi)), ACT.Copy)
-                nc.vector.scalar_tensor_tensor(
-                    gated[:, t, :], h_banks[t][:, lo:hi], gs16[:, t : t + 1], sg[c][:, t, :], ALU.mult, ALU.mult
-                )
-            z = sb.tile([P, HALF, PACK], BF16, name=f"z{c}", align_bytes=64)
+            z = sb.tile([P, HALF, PACK], BF16, name=f"z{c}", tag="z", align_bytes=64)
             nc.vector.tensor_tensor(
                 z[:].rearrange("p (c i) t -> p c t i", i=4),
-                gated[:].rearrange("p t (c i) -> p c t i", i=4),
+                gated[:, :, lo:hi].rearrange("p t (c i) -> p c t i", i=4),
                 fetched[:].rearrange("p t (c i) -> p c t i", i=4),
                 ALU.subtract,
             )
@@ -211,7 +209,7 @@ def tile_picked_ringekdepk_none_po_kernel(
             nc.vector.tensor_scalar(
                 h2[t][:, HALF:], h2_banks[1][t][:], 0.0625, top_first[:, col], ALU.mult, ALU.max, accum_out=top[:, col]
             )
-            nc.vector.tensor_scalar(exp_bias[:, col], top[:, col], tau_t[:, col], -1.0, ALU.mult, ALU.mult)
+            nc.gpsimd.tensor_scalar(exp_bias[:, col], top[:, col], minus_tau[:, col], 0.0, ALU.mult, ALU.add)
         for t in range(PACK):
             exp_and_multiply(0, t)
             exp_and_multiply(1, t)

@@ -58,62 +58,59 @@ def tile_picked_ringekdepk_none_po_kernel(
             queue.dma_start(col[:], src.rearrange("(p t) o -> p (t o)", t=PACK))
             return col
 
-        def load_scales(src, name):
-            table = sb.tile([P, TABLE], U8, name=name, align_bytes=64)
-            rows = src[0].bitcast(I32)
-            nc.sync.dma_start(table[:].bitcast(I32), rows.unsqueeze(1).to_broadcast([16, 8, TABLE // 4]))
-            return table
+        x_sc_table = sb.tile([P, TABLE // 4], I32, align_bytes=64)
+        nc.vector.memset(x_sc_table[:], 0)
+        d_sc_words = sb.tile([P, S // 4], I32, align_bytes=64)
+        nc.vector.memset(d_sc_words[:], 0)
 
         k1_t = load_list(k1, "k1_t")
-        d_sc_table = load_scales(d_scales, "d_sc_table")
+        d_sc_table = reuse.tile([P, TABLE // 4], I32, align_bytes=64, offset=4 * TABLE)
+        nc.sync.dma_start(d_sc_table[:], d_scales[0].bitcast(I32).unsqueeze(1).to_broadcast([16, 8, TABLE // 4]))
         offs_t = load_list(offs, "offs_t")
-        x_sc_table = load_scales(x_scales, "x_sc_table")
+        n3_t = load_list(n3, "n3_t")
         n1_t = load_list(n1, "n1_t")
         sl_t = load_column(sl, "sl_t", nc.sync)
-        th_t = load_column(th, "th_t", nc.sync)
-        d_table = load_words(d_words, "d_table", 0)
         tabs = [load_tab(0, 8 * TABLE)]
+        d_table = load_words(d_words, "d_table", 0)
+        tabs.append(load_tab(1, 8 * TABLE + 4 * S))
         n2_t = load_list(n2, "n2_t")
-        n3_t = load_list(n3, "n3_t")
-        x_table = load_words(x_words, "x_table", 4 * TABLE)
+        x_sc_rows = x_scales[0].bitcast(I32)
+        for q in range(4):
+            nc.sync.dma_start(x_sc_table[32 * q : 32 * q + 4, :], x_sc_rows[4 * q : 4 * q + 4, :])
+        th_t = load_column(th, "th_t", nc.gpsimd)
         gs_t = load_column(gs, "gs_t", nc.gpsimd)
         tau_t = load_column(tau, "tau_t", nc.gpsimd)
 
         d_sc_picked = sb.tile([P, S], U8, align_bytes=64)
-        nc.vector.tensor_copy(d_sc_picked[:], d_sc_table[:].indirect(k1_t[:]))
-        x_sc_picked = sb.tile([P, S], U8, align_bytes=64)
-        nc.vector.tensor_copy(x_sc_picked[:], x_sc_table[:].indirect(offs_t[:]))
-        spread_sc = sb.tile([P, 2 * S], U8, align_bytes=64)
+        nc.vector.tensor_copy(d_sc_picked[:], d_sc_table[:].bitcast(U8).indirect(k1_t[:]))
+        x_table = load_words(x_words, "x_table", 4 * TABLE)
+        d_sc_dealt = sb.tile([P, S], U8, align_bytes=64)
         nc.vector.tensor_copy(
-            spread_sc[:, :S].rearrange("p (t c i) -> p c t i", t=PACK, i=16),
+            d_sc_dealt[:].rearrange("p (t c i) -> p c t i", t=PACK, i=16),
             d_sc_picked[:].rearrange("p (c i t) -> p c t i", t=PACK, i=16),
         )
-        nc.vector.tensor_copy(spread_sc[:, S:].bitcast(I32), x_sc_picked[:].bitcast(I32))
-        packed_sc = sb.tile([P, 2 * S // 4], I32, align_bytes=64)
-        nc.gpsimd.memset(packed_sc[:], 0)
         for q in range(4):
-            nc.sync.dma_start(packed_sc[32 * q : 32 * q + 4, :], spread_sc[32 * q : 32 * q + 32 : 8, :].bitcast(I32))
-        d_sc = packed_sc[:].bitcast(U8)[:, :S]
-        x_sc = packed_sc[:].bitcast(U8)[:, S:]
+            nc.sync.dma_start(d_sc_words[32 * q : 32 * q + 4, :], d_sc_dealt[32 * q : 32 * q + 32 : 8, :].bitcast(I32))
+        d_sc = d_sc_words[:].bitcast(U8)
 
         d_picked = sb.tile([P, S], U32, align_bytes=64)
         nc.vector.tensor_copy(d_picked[:], d_table[:].bitcast(U32).indirect(k1_t[:]))
-        tabs.extend(load_tab(t, 4 * S * (t - 1)) for t in range(1, PACK))
+        tabs.extend(load_tab(t, 4 * S * (t - 2)) for t in range(2, PACK))
+        x_sc = sb.tile([P, S], U8, align_bytes=64)
+        nc.vector.tensor_copy(x_sc[:], x_sc_table[:].bitcast(U8).indirect(offs_t[:]))
         d_codes = sb.tile([P, S], U32, align_bytes=64)
         nc.vector.tensor_copy(
             d_codes[:].rearrange("p (t c i) -> p c t i", t=PACK, i=4),
             d_picked[:].rearrange("p (c i t) -> p c t i", t=PACK, i=4),
         )
 
-        sig_bias = sb.tile([P, PACK], F32)
+        sig_bias = sb.tile([P, PACK], F32, tag="sig_bias")
         minus_th = sb.tile([P, PACK], F32)
         nc.gpsimd.tensor_scalar(minus_th[:], th_t[:], -1.0, 0.0, ALU.mult, ALU.add)
         nc.gpsimd.tensor_tensor(sig_bias[:], sl_t[:], minus_th[:], ALU.mult)
         gs16 = sb.tile([P, PACK], F32)
         nc.gpsimd.tensor_scalar(gs16[:], gs_t[:], 0.0625, 0.0, ALU.mult, ALU.add)
 
-        minus_tau = sb.tile([P, PACK], F32)
-        nc.scalar.activation(minus_tau[:], tau_t[:], ACT.Copy, scale=-1.0)
         x_codes = sb.tile([P, S], U32, align_bytes=64)
         nc.vector.tensor_copy(x_codes[:], x_table[:].bitcast(U32).indirect(offs_t[:]))
 
@@ -140,45 +137,55 @@ def tile_picked_ringekdepk_none_po_kernel(
                     scale=sl_t[:, t : t + 1],
                 )
 
+        minus_tau = sb.tile([P, PACK], F32, tag="sig_bias")
+        nc.scalar.activation(minus_tau[:], tau_t[:], ACT.Copy, scale=-1.0)
+
         h_banks = []
         half_h = []
         for t in range(PACK):
             bank = ps.tile([P, S], F32, name=f"h{t}", tag=f"bank{t}")
-            product(bank[:], t, x_codes[:], x_sc)
+            product(bank[:], t, x_codes[:], x_sc[:])
             h_banks.append(bank)
         for t in range(PACK):
             window = sb.tile([P, S], F32, name=f"half_h{t}", align_bytes=64)
-            nc.vector.tensor_scalar(window[:], h_banks[t][:], gs_t[:, t : t + 1], 0.03125, ALU.mult, ALU.mult)
+            nc.vector.tensor_scalar(window[:], h_banks[t][:], gs_t[:, t : t + 1], 0.0625, ALU.mult, ALU.mult)
             half_h.append(window)
         gated = sb.tile([P, PACK, S], F32, align_bytes=64)
         for t in range(PACK):
-            nc.vector.scalar_tensor_tensor(
-                gated[:, t, :], h_banks[t][:], gs16[:, t : t + 1], sg[:, t, :], ALU.mult, ALU.mult
-            )
+            if t < 2:
+                nc.gpsimd.tensor_tensor(gated[:, t, :], half_h[t][:], sg[:, t, :], ALU.mult)
+            else:
+                nc.vector.scalar_tensor_tensor(
+                    gated[:, t, :], h_banks[t][:], gs16[:, t : t + 1], sg[:, t, :], ALU.mult, ALU.mult
+                )
 
         z_codes = sb.tile([P, S], U32, align_bytes=64)
         z_sc = sb.tile([P, S], U8, align_bytes=64)
-        h2_banks = []
-        for c, (lo, hi) in enumerate(HALVES):
-            fetched = sb.tile([P, PACK, HALF], F32, name=f"fetched{c}", tag=("fetched0", "gs_t")[c], align_bytes=64)
+        fetched_first = sb.tile([P, PACK, HALF], F32, align_bytes=64)
+        fetched_rest = sb.tile([P, 2, PACK, HALF // 2], F32, tag="gs_t", align_bytes=64)
+        fetched = (fetched_first[:], fetched_rest[:, 0], fetched_rest[:, 1])
+        h2_banks = [
+            [ps.tile([P, HALF], F32, name=f"h2_{half}_{t}", tag=f"bank{(1 - half) * PACK + t}") for t in range(PACK)]
+            for half in range(2)
+        ]
+        for c, (lo, hi) in enumerate(OUT_CHUNKS):
             for t in range(PACK):
-                nc.scalar.activation(fetched[:, t, :], half_h[t][:].indirect(entries(n2_t, lo, hi)), ACT.Copy)
-            z = sb.tile([P, HALF, PACK], BF16, name=f"z{c}", tag="z", align_bytes=64)
+                nc.scalar.activation(
+                    fetched[c][:, t, :], half_h[t][:].indirect(entries(n2_t, lo, hi)), ACT.Copy, scale=0.5
+                )
+            z = sb.tile([P, hi - lo, PACK], BF16, name=f"z{c}", tag="z", align_bytes=64)
             nc.vector.tensor_tensor(
                 z[:].rearrange("p (c i) t -> p c t i", i=4),
                 gated[:, :, lo:hi].rearrange("p t (c i) -> p c t i", i=4),
-                fetched[:].rearrange("p t (c i) -> p c t i", i=4),
+                fetched[c].rearrange("p t (c i) -> p c t i", i=4),
                 ALU.subtract,
             )
             nc.vector.quantize_mx(
                 out=z_codes[:, lo:hi].bitcast(FP8X4), scales=z_sc[:, lo:hi], in_=z[:].rearrange("p j t -> p (j t)")
             )
-            banks = []
             for t in range(PACK):
-                bank = ps.tile([P, HALF], F32, name=f"h2_{c}_{t}", tag=f"bank{(1 - c) * PACK + t}")
-                product(bank[:], t, z_codes[:, lo:hi], z_sc[:, lo:hi])
-                banks.append(bank)
-            h2_banks.append(banks)
+                bank = h2_banks[lo // HALF][t]
+                product(bank[:, lo % HALF : lo % HALF + hi - lo], t, z_codes[:, lo:hi], z_sc[:, lo:hi])
 
         top_first = sb.tile([P, PACK], F32)
         top = sb.tile([P, PACK], F32, tag="top", align_bytes=64)
@@ -219,24 +226,33 @@ def tile_picked_ringekdepk_none_po_kernel(
         out_rows = out_0.rearrange("(p t) j -> p t j", t=PACK)
         out_words = out_1[0].rearrange("p c r -> p (c r)").bitcast(I32)
 
-        def hand_out(c):
+        rounded = [sb.tile([P, HALF, PACK], BF16, name=f"rounded{half}", align_bytes=64) for half in range(2)]
+
+        def store_and_round(c, copy):
             lo, hi = OUT_CHUNKS[c]
             nc.sync.dma_start(out_rows[:, :, lo:hi], y[c][:])
-            rounded = sb.tile([P, hi - lo, PACK], BF16, name=f"rounded{c}", align_bytes=64)
-            nc.vector.tensor_copy(
-                rounded[:].rearrange("p (c i) t -> p c t i", i=4), y[c][:].rearrange("p t (c i) -> p c t i", i=4)
+            copy(
+                rounded[lo // HALF][:, lo % HALF : lo % HALF + hi - lo, :].rearrange("p (c i) t -> p c t i", i=4),
+                y[c][:].rearrange("p t (c i) -> p c t i", i=4),
             )
+
+        def quantise_and_store(half):
+            lo, hi = HALVES[half]
             nc.vector.quantize_mx(
-                out=y_codes[:, lo:hi].bitcast(FP8X4), scales=y_sc[:, lo:hi], in_=rounded[:].rearrange("p j t -> p (j t)")
+                out=y_codes[:, lo:hi].bitcast(FP8X4),
+                scales=y_sc[:, lo:hi],
+                in_=rounded[half][:].rearrange("p j t -> p (j t)"),
             )
             nc.sync.dma_start(out_words[:, lo:hi], y_codes[:, lo:hi].bitcast(I32))
 
-        hand_out(0)
+        store_and_round(0, nc.vector.tensor_copy)
         ea.append(sb.tile([P, PACK, 128], F32, name="ea2", tag="top", align_bytes=64))
         for t in range(PACK):
             exp_and_multiply(2, t)
-        hand_out(1)
-        hand_out(2)
+        quantise_and_store(0)
+        store_and_round(1, nc.scalar.copy)
+        store_and_round(2, nc.scalar.copy)
+        quantise_and_store(1)
         out_sc_rows = out_2[0].bitcast(I32)
         for q in range(4):
             queue = nc.scalar if q % 2 == 0 else nc.sync

from contextlib import ExitStack

import concourse.mybir as mybir

F32 = mybir.dt.float32
BF16 = mybir.dt.bfloat16
I32 = mybir.dt.int32
U32 = mybir.dt.uint32
U16 = mybir.dt.uint16
U8 = mybir.dt.uint8
FP8X4 = mybir.dt.float8_e4m3fn_x4
ALU = mybir.AluOpType
ACT = mybir.ActivationFunctionType

P = 128
PACK = 4
TABLE = 2048
S = 512
HALF = S // 2
FLOPS = 2 * 2 * 512 * 512 * 512

HALVES = ((0, HALF), (HALF, S))
OUT_CHUNKS = ((0, 256), (256, 384), (384, 512))


def entries(lst, lo, hi):
    return lst[:, lo // 16 : hi // 16]


def tile_picked_ringekdepk_none_po_kernel(
    tc, x_words, x_scales, d_words, d_scales, tab, sl, th, gs, tau, offs, k1, n1, n2, n3, out_0, out_1, out_2
):
    nc = tc.nc
    with ExitStack() as ctx:
        sb = ctx.enter_context(tc.tile_pool(name="sb", bufs=1))
        reuse = ctx.enter_context(tc.tile_pool(name="reuse", bufs=1))
        ps = ctx.enter_context(tc.psum_pool(name="ps", bufs=1))

        def load_list(src, name):
            lst = sb.tile([P, S // 16], U16, name=name)
            nc.sync.dma_start(lst[:], src)
            return lst

        def load_words(src, name, offset):
            words = reuse.tile([P, TABLE], I32, name=name, align_bytes=64, offset=offset)
            nc.sync.dma_start(words[:], src[0].rearrange("p c r -> p (c r)").bitcast(I32))
            return words

        tab_rows = tab.rearrange("(p t) j -> p t j", t=PACK)

        def load_tab(t, offset):
            rows = reuse.tile([P, S], F32, name=f"tab{t}", align_bytes=64, offset=offset)
            nc.sync.dma_start(rows[:], tab_rows[:, t, :])
            return rows

        def load_column(src, name, queue):
            col = sb.tile([P, PACK], F32, name=name, tag=name, align_bytes=64)
            queue.dma_start(col[:], src.rearrange("(p t) o -> p (t o)", t=PACK))
            return col

        x_sc_table = sb.tile([P, TABLE // 4], I32, align_bytes=64)
        nc.vector.memset(x_sc_table[:], 0)
        d_sc_words = sb.tile([P, S // 4], I32, align_bytes=64)
        nc.vector.memset(d_sc_words[:], 0)

        k1_t = load_list(k1, "k1_t")
        d_sc_table = reuse.tile([P, TABLE // 4], I32, align_bytes=64, offset=4 * TABLE)
        nc.sync.dma_start(d_sc_table[:], d_scales[0].bitcast(I32).unsqueeze(1).to_broadcast([16, 8, TABLE // 4]))
        offs_t = load_list(offs, "offs_t")
        n3_t = load_list(n3, "n3_t")
        n1_t = load_list(n1, "n1_t")
        sl_t = load_column(sl, "sl_t", nc.sync)
        tabs = [load_tab(0, 8 * TABLE)]
        d_table = load_words(d_words, "d_table", 0)
        tabs.append(load_tab(1, 8 * TABLE + 4 * S))
        n2_t = load_list(n2, "n2_t")
        x_sc_rows = x_scales[0].bitcast(I32)
        for q in range(4):
            nc.sync.dma_start(x_sc_table[32 * q : 32 * q + 4, :], x_sc_rows[4 * q : 4 * q + 4, :])
        th_t = load_column(th, "th_t", nc.gpsimd)
        gs_t = load_column(gs, "gs_t", nc.gpsimd)
        tau_t = load_column(tau, "tau_t", nc.gpsimd)

        d_sc_picked = sb.tile([P, S], U8, align_bytes=64)
        nc.vector.tensor_copy(d_sc_picked[:], d_sc_table[:].bitcast(U8).indirect(k1_t[:]))
        x_table = load_words(x_words, "x_table", 4 * TABLE)
        d_sc_dealt = sb.tile([P, S], U8, align_bytes=64)
        nc.vector.tensor_copy(
            d_sc_dealt[:].rearrange("p (t c i) -> p c t i", t=PACK, i=16),
            d_sc_picked[:].rearrange("p (c i t) -> p c t i", t=PACK, i=16),
        )
        for q in range(4):
            nc.sync.dma_start(d_sc_words[32 * q : 32 * q + 4, :], d_sc_dealt[32 * q : 32 * q + 32 : 8, :].bitcast(I32))
        d_sc = d_sc_words[:].bitcast(U8)

        d_picked = sb.tile([P, S], U32, align_bytes=64)
        nc.vector.tensor_copy(d_picked[:], d_table[:].bitcast(U32).indirect(k1_t[:]))
        tabs.extend(load_tab(t, 4 * S * (t - 2)) for t in range(2, PACK))
        x_sc = sb.tile([P, S], U8, align_bytes=64)
        nc.vector.tensor_copy(x_sc[:], x_sc_table[:].bitcast(U8).indirect(offs_t[:]))
        d_codes = sb.tile([P, S], U32, align_bytes=64)
        nc.vector.tensor_copy(
            d_codes[:].rearrange("p (t c i) -> p c t i", t=PACK, i=4),
            d_picked[:].rearrange("p (c i t) -> p c t i", t=PACK, i=4),
        )

        sig_bias = sb.tile([P, PACK], F32, tag="sig_bias")
        minus_th = sb.tile([P, PACK], F32)
        nc.gpsimd.tensor_scalar(minus_th[:], th_t[:], -1.0, 0.0, ALU.mult, ALU.add)
        nc.gpsimd.tensor_tensor(sig_bias[:], sl_t[:], minus_th[:], ALU.mult)
        gs16 = sb.tile([P, PACK], F32)
        nc.gpsimd.tensor_scalar(gs16[:], gs_t[:], 0.0625, 0.0, ALU.mult, ALU.add)

        x_codes = sb.tile([P, S], U32, align_bytes=64)
        nc.vector.tensor_copy(x_codes[:], x_table[:].bitcast(U32).indirect(offs_t[:]))

        def product(bank, t, codes, scales):
            cols = slice(t * P, (t + 1) * P)
            nc.tensor.matmul_mx(
                out=bank,
                lhsT=d_codes[:, cols].bitcast(FP8X4),
                lhsT_scale=d_sc[:, cols],
                rhs=codes.bitcast(FP8X4),
                rhs_scale=scales,
                start=True,
                stop=True,
            )

        sg = sb.tile([P, PACK, S], F32, align_bytes=64)
        for t in range(PACK):
            for lo, hi in HALVES:
                nc.scalar.activation(
                    sg[:, t, lo:hi],
                    tabs[t][:].indirect(entries(n1_t, lo, hi)),
                    ACT.Sigmoid,
                    bias=sig_bias[:, t : t + 1],
                    scale=sl_t[:, t : t + 1],
                )

        minus_tau = sb.tile([P, PACK], F32, tag="sig_bias")
        nc.scalar.activation(minus_tau[:], tau_t[:], ACT.Copy, scale=-1.0)

        h_banks = []
        half_h = []
        for t in range(PACK):
            bank = ps.tile([P, S], F32, name=f"h{t}", tag=f"bank{t}")
            product(bank[:], t, x_codes[:], x_sc[:])
            h_banks.append(bank)
        for t in range(PACK):
            window = sb.tile([P, S], F32, name=f"half_h{t}", align_bytes=64)
            nc.vector.tensor_scalar(window[:], h_banks[t][:], gs_t[:, t : t + 1], 0.0625, ALU.mult, ALU.mult)
            half_h.append(window)
        gated = sb.tile([P, PACK, S], F32, align_bytes=64)
        for t in range(PACK):
            if t < 2:
                nc.gpsimd.tensor_tensor(gated[:, t, :], half_h[t][:], sg[:, t, :], ALU.mult)
            else:
                nc.vector.scalar_tensor_tensor(
                    gated[:, t, :], h_banks[t][:], gs16[:, t : t + 1], sg[:, t, :], ALU.mult, ALU.mult
                )

        z_codes = sb.tile([P, S], U32, align_bytes=64)
        z_sc = sb.tile([P, S], U8, align_bytes=64)
        fetched_first = sb.tile([P, PACK, HALF], F32, align_bytes=64)
        fetched_rest = sb.tile([P, 2, PACK, HALF // 2], F32, tag="gs_t", align_bytes=64)
        fetched = (fetched_first[:], fetched_rest[:, 0], fetched_rest[:, 1])
        h2_banks = [
            [ps.tile([P, HALF], F32, name=f"h2_{half}_{t}", tag=f"bank{(1 - half) * PACK + t}") for t in range(PACK)]
            for half in range(2)
        ]
        for c, (lo, hi) in enumerate(OUT_CHUNKS):
            for t in range(PACK):
                nc.scalar.activation(
                    fetched[c][:, t, :], half_h[t][:].indirect(entries(n2_t, lo, hi)), ACT.Copy, scale=0.5
                )
            z = sb.tile([P, hi - lo, PACK], BF16, name=f"z{c}", tag="z", align_bytes=64)
            nc.vector.tensor_tensor(
                z[:].rearrange("p (c i) t -> p c t i", i=4),
                gated[:, :, lo:hi].rearrange("p t (c i) -> p c t i", i=4),
                fetched[c].rearrange("p t (c i) -> p c t i", i=4),
                ALU.subtract,
            )
            nc.vector.quantize_mx(
                out=z_codes[:, lo:hi].bitcast(FP8X4), scales=z_sc[:, lo:hi], in_=z[:].rearrange("p j t -> p (j t)")
            )
            for t in range(PACK):
                bank = h2_banks[lo // HALF][t]
                product(bank[:, lo % HALF : lo % HALF + hi - lo], t, z_codes[:, lo:hi], z_sc[:, lo:hi])

        top_first = sb.tile([P, PACK], F32)
        top = sb.tile([P, PACK], F32, tag="top", align_bytes=64)
        exp_bias = sb.tile([P, PACK], F32)
        ea = [sb.tile([P, PACK, hi - lo], F32, name=f"ea{c}", align_bytes=64) for c, (lo, hi) in enumerate(OUT_CHUNKS[:2])]
        y = [sb.tile([P, PACK, hi - lo], F32, name=f"y{c}", align_bytes=64) for c, (lo, hi) in enumerate(OUT_CHUNKS)]
        h2 = [sb.tile([P, S], F32, name=f"h2_{t}", align_bytes=64) for t in range(PACK)]

        def exp_and_multiply(c, t):
            lo, hi = OUT_CHUNKS[c]
            nc.scalar.activation(
                ea[c][:, t, :],
                h2[t][:].indirect(entries(n3_t, lo, hi)),
                ACT.Exp,
                bias=exp_bias[:, t : t + 1],
                scale=tau_t[:, t : t + 1],
            )
            bank = h2_banks[lo // HALF][t]
            nc.vector.scalar_tensor_tensor(
                y[c][:, t, :], bank[:, lo % HALF : lo % HALF + hi - lo], 0.125, ea[c][:, t, :], ALU.mult, ALU.mult
            )

        for t in range(PACK):
            col = slice(t, t + 1)
            nc.vector.tensor_scalar(
                h2[t][:, :HALF], h2_banks[0][t][:], 0.0625, None, ALU.mult, ALU.max, accum_out=top_first[:, col]
            )
            nc.vector.tensor_scalar(
                h2[t][:, HALF:], h2_banks[1][t][:], 0.0625, top_first[:, col], ALU.mult, ALU.max, accum_out=top[:, col]
            )
            nc.gpsimd.tensor_scalar(exp_bias[:, col], top[:, col], minus_tau[:, col], 0.0, ALU.mult, ALU.add)
        for t in range(PACK):
            exp_and_multiply(0, t)
            exp_and_multiply(1, t)

        y_codes = sb.tile([P, S], U32, align_bytes=64)
        y_sc = sb.tile([P, S], U8, align_bytes=64)
        out_rows = out_0.rearrange("(p t) j -> p t j", t=PACK)
        out_words = out_1[0].rearrange("p c r -> p (c r)").bitcast(I32)

        rounded = [sb.tile([P, HALF, PACK], BF16, name=f"rounded{half}", align_bytes=64) for half in range(2)]

        def store_and_round(c, copy):
            lo, hi = OUT_CHUNKS[c]
            nc.sync.dma_start(out_rows[:, :, lo:hi], y[c][:])
            copy(
                rounded[lo // HALF][:, lo % HALF : lo % HALF + hi - lo, :].rearrange("p (c i) t -> p c t i", i=4),
                y[c][:].rearrange("p t (c i) -> p c t i", i=4),
            )

        def quantise_and_store(half):
            lo, hi = HALVES[half]
            nc.vector.quantize_mx(
                out=y_codes[:, lo:hi].bitcast(FP8X4),
                scales=y_sc[:, lo:hi],
                in_=rounded[half][:].rearrange("p j t -> p (j t)"),
            )
            nc.sync.dma_start(out_words[:, lo:hi], y_codes[:, lo:hi].bitcast(I32))

        store_and_round(0, nc.vector.tensor_copy)
        ea.append(sb.tile([P, PACK, 128], F32, name="ea2", tag="top", align_bytes=64))
        for t in range(PACK):
            exp_and_multiply(2, t)
        quantise_and_store(0)
        store_and_round(1, nc.scalar.copy)
        store_and_round(2, nc.scalar.copy)
        quantise_and_store(1)
        out_sc_rows = out_2[0].bitcast(I32)
        for q in range(4):
            queue = nc.scalar if q % 2 == 0 else nc.sync
            queue.dma_start(out_sc_rows[4 * q : 4 * q + 4, :], y_sc[:].bitcast(I32)[32 * q : 32 * q + 4, :])
